import numpy as np
import ml_dtypes


def mxq(x, axis, fmt="e4m3"):
    dtype, down = {"e4m3": (ml_dtypes.float8_e4m3fn, 7), "e5m2": (ml_dtypes.float8_e5m2, 14)}[fmt]
    v = np.moveaxis(np.asarray(x, np.float32).astype(ml_dtypes.bfloat16).astype(np.float64), axis, -1)
    blocks = v.reshape(v.shape[:-1] + (-1, 32))
    amax = np.abs(blocks).max(-1, keepdims=True)
    byte = np.maximum(np.where(amax > 0, np.frexp(amax)[1] - 1 + 127, 0) - down, 1)
    scale = np.exp2(byte - 127.0)
    codes = (blocks / scale).astype(np.float32).astype(dtype).astype(np.float64)
    return np.moveaxis((codes * scale).reshape(v.shape), -1, axis)


WIDE = False


def mx_kscale(k):
    if not WIDE:
        return np.ones(k)
    levels = np.array([10, -10, 5, -5, 0])
    if k % 512:
        return np.exp2(np.random.permutation(np.resize(levels, k // 32))).repeat(32)
    a = np.empty((k // 512, 16))
    for p in range(k // 512):
        a[p, :8] = np.random.permutation(np.resize(levels, 8))
        for g in range(8):
            far = levels[np.abs(levels - a[p, g]) >= 10]
            a[p, g + 8] = far[np.random.randint(len(far))]
    return np.exp2(a.ravel()).repeat(32)


def f64(x):
    return np.asarray(x).astype(np.float64)


def striped(idx):
    return np.tile(idx.reshape(-1, 16).T, (8, 1)).astype(np.uint16)


def unstriped(offs):
    return offs[:16].T.reshape(-1).astype(np.int64)


def striped8(idx):
    return np.concatenate([x.reshape(-1, 16).T for x in idx]).astype(np.uint16)


def runs(offs, k):
    lists = np.stack([offs[16 * r : 16 * r + 16].T.reshape(-1) for r in range(8)]).astype(np.int64)
    return lists[np.arange(k) % 512 // 64]


def pack_weight(w):
    k, n = w.shape
    w = f64(np.asarray(w, np.float32).astype(ml_dtypes.bfloat16)).reshape(k // 32, 32, n)
    amax = np.abs(w).max(1)
    byte = np.clip(np.where(amax > 0, np.frexp(amax)[1] - 1 + 127 - 7, 1), 1, 254)
    scaled = (w * np.exp2(127.0 - byte)[:, None, :]).reshape(k, n).astype(np.float32)
    words = np.ascontiguousarray(scaled.reshape(k // 512, 128, 4, n).transpose(0, 1, 3, 2)).astype(ml_dtypes.float8_e4m3fn).view(np.uint8)
    return words, np.ascontiguousarray(byte.astype(np.uint8).reshape(k // 512, 16, n))


def unpack_weight(words, scales):
    g, p, n, _ = words.shape
    vals = np.ascontiguousarray(words).view(ml_dtypes.float8_e4m3fn).astype(np.float64) * np.repeat(np.exp2(scales.astype(np.float64) - 127.0), 8, axis=1)[..., None]
    return vals.transpose(0, 1, 3, 2).reshape(g * 512, n)


E2M1 = np.array([0.0, 0.5, 1.0, 1.5, 2.0, 3.0, 4.0, 6.0, -0.0, -0.5, -1.0, -1.5, -2.0, -3.0, -4.0, -6.0])


def pack_fp4(w):
    k, n = w.shape
    w = f64(np.asarray(w, np.float32).astype(ml_dtypes.bfloat16)).reshape(k // 32, 32, n)
    amax = np.abs(w).max(1)
    mant, ex = np.frexp(amax / 6.0)
    byte = np.clip(np.where(amax > 0, np.where(mant > 0.5, ex, ex - 1) + 127, 1), 1, 254)
    scaled = (w * np.exp2(127.0 - byte)[:, None, :]).reshape(k, n).astype(np.float32)
    c = np.ascontiguousarray(scaled.reshape(k // 512, 128, 4, n).transpose(0, 1, 3, 2)).astype(ml_dtypes.float4_e2m1fn).view(np.uint8) & 0xF
    words = (c[..., 0::2] | (c[..., 1::2] << 4)).reshape(k // 512, 128, 2 * n)
    return np.ascontiguousarray(words), np.ascontiguousarray(byte.astype(np.uint8).reshape(k // 512, 16, n))


def unpack_fp4(words, scales):
    g, _, n = scales.shape
    words = np.ascontiguousarray(words).reshape(g, 128, n, 2)
    nib = np.empty((g, 128, n, 4), np.uint8)
    nib[..., 0::2] = words & 0xF
    nib[..., 1::2] = words >> 4
    vals = E2M1[nib] * np.repeat(np.exp2(scales.astype(np.float64) - 127.0), 8, axis=1)[..., None]
    return vals.transpose(0, 1, 3, 2).reshape(g * 512, n)


def planes(y):
    n, m = y.shape
    v = y.astype(np.float32).astype(ml_dtypes.bfloat16).astype(np.float64).reshape(n // 32, 32, m)
    top = np.abs(v).max(1)
    byte = np.clip(np.where(top > 0, np.frexp(top)[1] - 1 + 127 - 7, 1), 1, 254)
    codes = (v * np.exp2(127.0 - byte)[:, None, :]).reshape(n, m).astype(np.float32).astype(ml_dtypes.float8_e4m3fn).view(np.uint8)
    words = codes.reshape(n // 512, 128, 4, m).transpose(0, 1, 3, 2)
    return np.ascontiguousarray(words), np.ascontiguousarray(byte.astype(np.uint8).reshape(n // 512, 16, m))


K, T, S, N, H, W = 512, 2048, 512, 512, 512, 256


def setup_inputs():
    n = np.random.standard_normal
    s = mx_kscale(K)[:, None]
    u = mx_kscale(H)
    packed_xT = pack_weight(n((K, T)) * s)
    packed_w1 = pack_fp4(n((K, H)) / np.sqrt(K) / s)
    packed_w2 = pack_fp4(n((K, H)) / np.sqrt(K) / s)
    packed_w3 = pack_fp4(n((H, H)) / np.sqrt(H) / u[:, None])
    packed_w4 = pack_fp4(n((H, N)) / np.sqrt(H) / u[:, None])
    perm = np.stack([np.random.permutation(S) for _ in range(8)])
    return {
        "x_words": packed_xT[0],
        "x_scales": packed_xT[1],
        "w1_words": packed_w1[0],
        "w1_scales": packed_w1[1],
        "w2_words": packed_w2[0],
        "w2_scales": packed_w2[1],
        "gn": (np.random.uniform(0.5, 1.5, (H, 1)) * u[:, None]).astype(np.float32),
        "w3_words": packed_w3[0],
        "w3_scales": packed_w3[1],
        "res": (1.5 * n((N, S))).astype(np.float32),
        "w4_words": packed_w4[0],
        "w4_scales": packed_w4[1],
        "offs": striped(np.random.permutation(T)[:S]),
        "two": striped(np.random.permutation(T)[:S]),
        "n1": striped8(perm[:, :W]),
        "n2": striped8(perm[:, W:]),
        "n3": striped8(np.stack([np.random.permutation(S) for _ in range(8)])),
        "n4": striped8(np.stack([np.random.permutation(S) for _ in range(8)])),
    }


def reference(x_words, x_scales, w1_words, w1_scales, w2_words, w2_scales, gn, w3_words, w3_scales, res, w4_words, w4_scales, offs, two, n1, n2, n3, n4):
    xq = unpack_weight(x_words, x_scales)[:, unstriped(offs)]
    y = unpack_fp4(w1_words, w1_scales).T @ xq
    pb = y[np.arange(H)[:, None], runs(n2, H)]
    pa = y[np.arange(H)[:, None], runs(n1, H)]
    rb = pb - (0.5 * pa)
    ra = np.sqrt((pa) ** 2 + (pb) ** 2 + 0.25)
    ds = np.zeros((H, S))
    ds[np.arange(H)[:, None], runs(n1, H)] = ra
    dt = ds.copy()
    dt[np.arange(H)[:, None], runs(n2, H)] = rb
    z = f64(gn) * dt
    h = unpack_fp4(w3_words, w3_scales).T @ mxq(z, 0, "e4m3")
    x_two = unpack_weight(x_words, x_scales)[:, unstriped(two)]
    d = unpack_fp4(w2_words, w2_scales).T @ x_two
    z2 = f64(gn) * (h[np.arange(H)[:, None], runs(n3, H)] - (np.tanh(d) * (d[np.arange(H)[:, None], runs(n4, H)])))
    out_0 = f64(res) + (unpack_fp4(w4_words, w4_scales).T @ mxq(z2, 0, "e4m3"))
    return (out_0,) + planes(out_0)

@@ -1,0 +1,221 @@
+from contextlib import ExitStack
+
+import concourse.mybir as mybir
+
+F32 = mybir.dt.float32
+BF16 = mybir.dt.bfloat16
+I32 = mybir.dt.int32
+U32 = mybir.dt.uint32
+U16 = mybir.dt.uint16
+U8 = mybir.dt.uint8
+FP8X4 = mybir.dt.float8_e4m3fn_x4
+FP4X4 = mybir.dt.float4_e2m1fn_x4
+ACT = mybir.ActivationFunctionType
+ALU = mybir.AluOpType
+
+P = 128
+PACK = 4
+T = 2048
+S = 512
+W = 256
+FLOPS = 4 * 2 * 512 * 512 * 512
+CHUNKS = ((0, 256), (256, 128), (384, 128))
+
+
+def tile_picked_midsoftbpolar_none_po_kernel(
+    tc, x_words, x_scales, w1_words, w1_scales, w2_words, w2_scales, gn, w3_words, w3_scales, res,
+    w4_words, w4_scales, offs, two, n1, n2, n3, n4, out_0, out_1, out_2,
+):
+    nc = tc.nc
+    with ExitStack() as ctx:
+        lists = ctx.enter_context(tc.tile_pool(name="lists", bufs=1))
+        sb = ctx.enter_context(tc.tile_pool(name="sb", bufs=1))
+        psum = ctx.enter_context(tc.psum_pool(name="psum", bufs=1))
+
+        def load_list(src, name):
+            tile = lists.tile(list(src.shape), U16, name=name)
+            nc.sync.dma_start(tile[:], src)
+            return tile
+
+        def load_scale_rows(tile, src):
+            for q in range(4):
+                nc.sync.dma_start(
+                    out=tile[32 * q : 32 * q + 4, :].bitcast(I32), in_=src[0, 4 * q : 4 * q + 4, :].bitcast(I32)
+                )
+
+        def load_weight(words, scales, name, tag):
+            raw_words = sb.tile([P, 2 * S], U8, name=name + "_raw_words", tag=tag + "_words")
+            nc.sync.dma_start(out=raw_words[:].bitcast(I32), in_=words[0].bitcast(I32))
+            raw_scales = sb.tile([P, S], U8, name=name + "_raw_scales")
+            nc.gpsimd.memset(raw_scales[:].bitcast(I32), 0)
+            load_scale_rows(raw_scales, scales)
+            return raw_words, raw_scales
+
+        def deal_weight(raw, name):
+            raw_words, raw_scales = raw
+            words = sb.tile([P, PACK, 2 * P], U8, name=name + "_words", align_bytes=64)
+            scales = sb.tile([P, PACK, P], U8, name=name + "_scales", align_bytes=64)
+            nc.vector.tensor_copy(
+                out=words[:].rearrange("p t (m b) -> p t m b", b=2),
+                in_=raw_words[:].rearrange("p (m t b) -> p t m b", t=PACK, b=2),
+            )
+            nc.vector.tensor_copy(out=scales[:], in_=raw_scales[:].rearrange("p (m t) -> p t m", t=PACK))
+            return words, scales
+
+        def product(out, weight, t, codes, scales):
+            nc.tensor.matmul_mx(
+                out=out, lhsT=weight[0][:, t, :].bitcast(FP4X4), lhsT_scale=weight[1][:, t, :],
+                rhs=codes.bitcast(FP8X4), rhs_scale=scales, start=True, stop=True,
+            )
+
+        def interleave(copy, dst, src):
+            copy(out=dst.rearrange("p (c i) t -> p c t i", i=4), in_=src.rearrange("p t (c i) -> p c t i", i=4))
+
+        warm = sb.tile([P, 2], F32, name="warm")
+        nc.gpsimd.memset(warm[:, 0:1], 0.0)
+        nc.scalar.activation(warm[:, 1:2], warm[:, 0:1], ACT.Tanh)
+
+        xs = sb.tile([P, T], U8, name="xs")
+        nc.vector.memset(xs[:].bitcast(I32), 0)
+        offs_t = load_list(offs, "offs_t")
+        load_scale_rows(xs, x_scales)
+        two_t = load_list(two, "two_t")
+        w1_raw = load_weight(w1_words, w1_scales, "w1", "raw_a")
+        xw = sb.tile([P, T], U32, name="xw", tag="big")
+        nc.sync.dma_start(out=xw[:].bitcast(I32), in_=x_words[0].rearrange("p n t -> p (n t)").bitcast(I32))
+        w2_raw = load_weight(w2_words, w2_scales, "w2", "raw_b")
+        n1_t = load_list(n1, "n1_t")
+        n2_t = load_list(n2, "n2_t")
+        gain = sb.tile([P, PACK], F32, name="gain")
+        nc.sync.dma_start(out=gain[:], in_=gn.rearrange("(p t) o -> p (t o)", t=PACK))
+
+        xa_scales = sb.tile([P, S], U8, name="xa_scales", align_bytes=64)
+        xb_scales = sb.tile([P, S], U8, name="xb_scales", align_bytes=64)
+        xa_words = sb.tile([P, S], U32, name="xa_words", align_bytes=64)
+        xb_words = sb.tile([P, S], U32, name="xb_words", align_bytes=64)
+        nc.vector.tensor_copy(xa_scales[:], xs[:].indirect(offs_t[:]))
+        nc.vector.tensor_copy(xb_scales[:], xs[:].indirect(two_t[:]))
+        w1 = deal_weight(w1_raw, "w1")
+        nc.vector.tensor_copy(xa_words[:], xw[:].indirect(offs_t[:]))
+        nc.vector.tensor_copy(xb_words[:], xw[:].indirect(two_t[:]))
+        w2 = deal_weight(w2_raw, "w2")
+
+        w3_raw = load_weight(w3_words, w3_scales, "w3", "raw_a")
+        w4_raw = load_weight(w4_words, w4_scales, "w4", "raw_b")
+        n3_t = load_list(n3, "n3_t")
+        n4_t = load_list(n4, "n4_t")
+        res_t = sb.tile([P, PACK, S], F32, name="res_t", tag="big")
+        nc.sync.dma_start(out=res_t[:], in_=res.rearrange("(p t) j -> p t j", t=PACK))
+
+        y = []
+        for t in range(PACK):
+            bank = psum.tile([P, S], F32, name=f"y_bank{t}", tag=f"bank{t}")
+            product(bank[:], w1, t, xa_words[:], xa_scales[:])
+            y_t = sb.tile([P, S], F32, name=f"y{t}")
+            nc.scalar.copy(y_t[:], bank[:])
+            y.append(y_t)
+        tanh_d = sb.tile([P, PACK, S], F32, name="tanh_d")
+        d_banks = []
+        for t in range(PACK):
+            bank = psum.tile([P, S], F32, name=f"d_bank{t}", tag=f"bank{PACK + t}")
+            product(bank[:], w2, t, xb_words[:], xb_scales[:])
+            nc.scalar.activation(tanh_d[:, t, :], bank[:], ACT.Tanh)
+            d_banks.append(bank)
+
+        half_a = sb.tile([P, PACK, W], F32, name="half_a")
+        pb = sb.tile([P, PACK, W], F32, name="pb")
+        for t in range(PACK):
+            nc.vector.tensor_scalar(half_a[:, t, :], y[t][:].indirect(n1_t[:]), -0.5, 0.0, ALU.mult, ALU.add)
+            nc.vector.tensor_copy(pb[:, t, :], y[t][:].indirect(n2_t[:]))
+        w3 = deal_weight(w3_raw, "w3")
+        w4 = deal_weight(w4_raw, "w4")
+
+        sq_a = sb.tile([P, PACK, W], F32, name="sq_a")
+        sq_b = sb.tile([P, PACK, W], F32, name="sq_b")
+        nc.scalar.activation(sq_a[:], half_a[:], ACT.Square, scale=2.0)
+        nc.scalar.activation(sq_b[:], pb[:], ACT.Square)
+
+        dt = [sb.tile([P, S], F32, name=f"dt{t}") for t in range(PACK)]
+        sq = sb.tile([P, PACK, W], F32, name="sq")
+        ra = sb.tile([P, PACK, W], F32, name="ra", tag="ra_u")
+        for t in range(PACK):
+            nc.vector.tensor_tensor(dt[t][:].indirect(n2_t[:]), pb[:, t, :], half_a[:, t, :], ALU.add)
+            if t == 1:
+                nc.vector.scalar_tensor_tensor(sq[:], sq_a[:], 0.25, sq_b[:], ALU.add, ALU.add)
+                nc.scalar.activation(ra[:], sq[:], ACT.Sqrt)
+        gd = []
+        for t in range(PACK):
+            gd_t = sb.tile([P, S], F32, name=f"gd{t}")
+            nc.scalar.activation(gd_t[:], d_banks[t][:], ACT.Copy, scale=gain[:, t : t + 1])
+            gd.append(gd_t)
+
+        z = sb.tile([P, S, PACK], BF16, name="z", tag="z_u", align_bytes=64)
+        for t in range(PACK):
+            nc.vector.tensor_copy(dt[t][:].indirect(n1_t[:]), ra[:, t, :])
+            nc.scalar.activation(z[:, :, t], dt[t][:], ACT.Copy, scale=gain[:, t : t + 1])
+
+        def gated(dst, t):
+            for c in range(0, S, W):
+                nc.vector.tensor_tensor(
+                    dst[:, c : c + W], gd[t][:].indirect(n4_t[:, c // 16 : (c + W) // 16]), tanh_d[:, t, c : c + W], ALU.mult
+                )
+
+        u_first = sb.tile([P, S], F32, name="u_first", tag="ra_u")
+        gated(u_first, 0)
+        z_codes = sb.tile([P, S], U32, name="z_codes", align_bytes=64)
+        z_scales = sb.tile([P, S], U8, name="z_scales", align_bytes=64)
+        nc.vector.quantize_mx(out=z_codes[:].bitcast(FP8X4), scales=z_scales[:], in_=z[:].rearrange("p j t -> p (j t)"))
+        u_rest = sb.tile([P, PACK - 1, S], F32, name="u_rest", tag="z_u", align_bytes=64)
+        u = [u_first[:]] + [u_rest[:, t, :] for t in range(PACK - 1)]
+        for t in range(1, PACK):
+            gated(u[t], t)
+
+        gh = []
+        for t in range(PACK):
+            bank = psum.tile([P, S], F32, name=f"h_bank{t}", tag=f"bank{t}")
+            product(bank[:], w3, t, z_codes[:], z_scales[:])
+            gh_t = sb.tile([P, S], F32, name=f"gh{t}")
+            nc.scalar.activation(gh_t[:], bank[:], ACT.Copy, scale=gain[:, t : t + 1])
+            gh.append(gh_t)
+
+        out_scales = sb.tile([P, S], U8, name="out_scales", align_bytes=64)
+        out_rows = out_0.rearrange("(p t) j -> p t j", t=PACK)
+        out_words = out_1[0].rearrange("p n t -> p (n t)").bitcast(I32)
+        next_bank = PACK
+        for index, (c0, n) in enumerate(CHUNKS):
+            last = index == len(CHUNKS) - 1
+            copy = nc.vector.tensor_copy if last else nc.scalar.copy
+            cols = slice(c0, c0 + n)
+            z2f = sb.tile([P, PACK, n], F32, name=f"z2f{index}")
+            for t in range(PACK):
+                nc.vector.tensor_tensor(
+                    z2f[:, t, :], gh[t][:].indirect(n3_t[:, c0 // 16 : (c0 + n) // 16]), u[t][:, cols], ALU.subtract
+                )
+            z2 = sb.tile([P, n, PACK], BF16, name=f"z2{index}", align_bytes=64)
+            interleave(copy, z2[:], z2f[:])
+            z2_codes = sb.tile([P, n], U32, name=f"z2_codes{index}", align_bytes=64)
+            z2_scales = sb.tile([P, n], U8, name=f"z2_scales{index}", align_bytes=64)
+            nc.vector.quantize_mx(out=z2_codes[:].bitcast(FP8X4), scales=z2_scales[:], in_=z2[:].rearrange("p j t -> p (j t)"))
+            result = sb.tile([P, PACK, n], F32, name=f"result{index}")
+            per_bank = S // n
+            for t0 in range(0, PACK, per_bank):
+                bank = psum.tile([P, per_bank, n], F32, name=f"o_bank{index}_{t0}", tag=f"bank{next_bank}")
+                next_bank = next_bank + 1
+                for t in range(t0, t0 + per_bank):
+                    product(bank[:, t - t0, :], w4, t, z2_codes[:], z2_scales[:])
+                nc.vector.tensor_tensor(
+                    result[:, t0 : t0 + per_bank, :], bank[:], res_t[:, t0 : t0 + per_bank, cols], ALU.add
+                )
+            nc.sync.dma_start(out=out_rows[:, :, cols], in_=result[:])
+            rounded = sb.tile([P, n, PACK], BF16, name=f"rounded{index}", align_bytes=64)
+            interleave(copy, rounded[:], result[:])
+            out_codes = sb.tile([P, n], U32, name=f"out_codes{index}", align_bytes=64)
+            nc.vector.quantize_mx(
+                out=out_codes[:].bitcast(FP8X4), scales=out_scales[:, cols], in_=rounded[:].rearrange("p j t -> p (j t)")
+            )
+            nc.sync.dma_start(out=out_words[:, cols], in_=out_codes[:].bitcast(I32))
+        for q in range(4):
+            queue = nc.sync if q % 2 == 0 else nc.scalar
+            queue.dma_start(
+                out=out_2[0, 4 * q : 4 * q + 4, :].bitcast(I32), in_=out_scales[32 * q : 32 * q + 4, :].bitcast(I32)
+            )

@@ -1,6 +1,7 @@
 from contextlib import ExitStack
 
 import concourse.mybir as mybir
+from concourse.masks import make_identity
 
 F32 = mybir.dt.float32
 BF16 = mybir.dt.bfloat16
@@ -43,24 +44,28 @@ def tile_picked_midsoftbpolar_none_po_kernel(
                     out=tile[32 * q : 32 * q + 4, :].bitcast(I32), in_=src[0, 4 * q : 4 * q + 4, :].bitcast(I32)
                 )
 
-        def load_weight(words, scales, name, tag):
-            raw_words = sb.tile([P, 2 * S], U8, name=name + "_raw_words", tag=tag + "_words")
-            nc.sync.dma_start(out=raw_words[:].bitcast(I32), in_=words[0].bitcast(I32))
-            raw_scales = sb.tile([P, S], U8, name=name + "_raw_scales")
-            nc.gpsimd.memset(raw_scales[:].bitcast(I32), 0)
-            load_scale_rows(raw_scales, scales)
-            return raw_words, raw_scales
+        def load_words(src, name):
+            tile = sb.tile([P, 2 * S], U8, name=name, align_bytes=64)
+            nc.sync.dma_start(out=tile[:].bitcast(I32), in_=src[0].bitcast(I32))
+            return tile
 
-        def deal_weight(raw, name):
-            raw_words, raw_scales = raw
-            words = sb.tile([P, PACK, 2 * P], U8, name=name + "_words", align_bytes=64)
-            scales = sb.tile([P, PACK, P], U8, name=name + "_scales", align_bytes=64)
+        def zeroed(name, width):
+            tile = sb.tile([P, width], U8, name=name, align_bytes=64)
+            nc.gpsimd.memset(tile[:].bitcast(I32), 0)
+            return tile
+
+        def deal_words(raw, name):
+            words = sb.tile([P, PACK, 2 * P], U8, name=name, align_bytes=64)
             nc.vector.tensor_copy(
                 out=words[:].rearrange("p t (m b) -> p t m b", b=2),
-                in_=raw_words[:].rearrange("p (m t b) -> p t m b", t=PACK, b=2),
+                in_=raw[:].rearrange("p (m t b) -> p t m b", t=PACK, b=2),
             )
-            nc.vector.tensor_copy(out=scales[:], in_=raw_scales[:].rearrange("p (m t) -> p t m", t=PACK))
-            return words, scales
+            return words
+
+        def deal_scales(raw, name):
+            scales = sb.tile([P, PACK, P], U8, name=name, align_bytes=64)
+            nc.vector.tensor_copy(out=scales[:], in_=raw[:].rearrange("p (m t) -> p t m", t=PACK))
+            return scales
 
         def product(out, weight, t, codes, scales):
             nc.tensor.matmul_mx(
@@ -71,39 +76,62 @@ def tile_picked_midsoftbpolar_none_po_kernel(
         def interleave(copy, dst, src):
             copy(out=dst.rearrange("p (c i) t -> p c t i", i=4), in_=src.rearrange("p t (c i) -> p c t i", i=4))
 
-        warm = sb.tile([P, 2], F32, name="warm")
-        nc.gpsimd.memset(warm[:, 0:1], 0.0)
-        nc.scalar.activation(warm[:, 1:2], warm[:, 0:1], ACT.Tanh)
-
-        xs = sb.tile([P, T], U8, name="xs")
-        nc.vector.memset(xs[:].bitcast(I32), 0)
         offs_t = load_list(offs, "offs_t")
-        load_scale_rows(xs, x_scales)
-        two_t = load_list(two, "two_t")
-        w1_raw = load_weight(w1_words, w1_scales, "w1", "raw_a")
+        w1_raw = load_words(w1_words, "w1_raw")
+        w2_raw = load_words(w2_words, "w2_raw")
+        w3_raw = load_words(w3_words, "w3_raw")
+        w4_raw = load_words(w4_words, "w4_raw")
         xw = sb.tile([P, T], U32, name="xw", tag="big")
         nc.sync.dma_start(out=xw[:].bitcast(I32), in_=x_words[0].rearrange("p n t -> p (n t)").bitcast(I32))
-        w2_raw = load_weight(w2_words, w2_scales, "w2", "raw_b")
+        xs = zeroed("xs", T)
+        load_scale_rows(xs, x_scales)
+        ws_raw = zeroed("ws_raw", S)
+        load_scale_rows(ws_raw, w1_scales)
+        nc.sync.dma_start(out=ws_raw[68:84, :].bitcast(I32), in_=w2_scales[0].bitcast(I32))
+        nc.sync.dma_start(out=ws_raw[4:20, :].bitcast(I32), in_=w3_scales[0].bitcast(I32))
+        nc.sync.dma_start(out=ws_raw[36:52, :].bitcast(I32), in_=w4_scales[0].bitcast(I32))
+        two_t = load_list(two, "two_t")
         n1_t = load_list(n1, "n1_t")
         n2_t = load_list(n2, "n2_t")
         gain = sb.tile([P, PACK], F32, name="gain")
         nc.sync.dma_start(out=gain[:], in_=gn.rearrange("(p t) o -> p (t o)", t=PACK))
-
-        xa_scales = sb.tile([P, S], U8, name="xa_scales", align_bytes=64)
-        xb_scales = sb.tile([P, S], U8, name="xb_scales", align_bytes=64)
-        xa_words = sb.tile([P, S], U32, name="xa_words", align_bytes=64)
-        xb_words = sb.tile([P, S], U32, name="xb_words", align_bytes=64)
-        nc.vector.tensor_copy(xa_scales[:], xs[:].indirect(offs_t[:]))
-        nc.vector.tensor_copy(xb_scales[:], xs[:].indirect(two_t[:]))
-        w1 = deal_weight(w1_raw, "w1")
-        nc.vector.tensor_copy(xa_words[:], xw[:].indirect(offs_t[:]))
-        nc.vector.tensor_copy(xb_words[:], xw[:].indirect(two_t[:]))
-        w2 = deal_weight(w2_raw, "w2")
-
-        w3_raw = load_weight(w3_words, w3_scales, "w3", "raw_a")
-        w4_raw = load_weight(w4_words, w4_scales, "w4", "raw_b")
         n3_t = load_list(n3, "n3_t")
         n4_t = load_list(n4, "n4_t")
+        identity = sb.tile([P, P], F32, name="identity")
+        make_identity(nc, identity[:])
+
+        quarter = sb.tile([P, 1], F32, name="quarter")
+        nc.gpsimd.memset(quarter[:], 0.25)
+        warm = sb.tile([P, 1], F32, name="warm")
+        nc.scalar.activation(warm[:], quarter[:], ACT.Sqrt)
+
+        xa_scales = sb.tile([P, S], U8, name="xa_scales", align_bytes=64)
+        xa_words = sb.tile([P, S], U32, name="xa_words", align_bytes=64)
+        w1_dealt = deal_words(w1_raw, "w1_dealt")
+        w2_dealt = deal_words(w2_raw, "w2_dealt")
+        w3_dealt = deal_words(w3_raw, "w3_dealt")
+        w4_dealt = deal_words(w4_raw, "w4_dealt")
+        nc.vector.tensor_copy(xa_words[:], xw[:].indirect(offs_t[:]))
+        nc.vector.tensor_copy(xa_scales[:], xs[:].indirect(offs_t[:]))
+        ws_dealt = deal_scales(ws_raw, "ws_dealt")
+        w1 = (w1_dealt, ws_dealt)
+        xb_scales = sb.tile([P, S], U8, name="xb_scales", align_bytes=64)
+        nc.vector.tensor_copy(xb_scales[:], xs[:].indirect(two_t[:]))
+        xb_words = sb.tile([P, S], U32, name="xb_words", align_bytes=64)
+        nc.vector.tensor_copy(xb_words[:], xw[:].indirect(two_t[:]))
+
+        def placed_scales(first_row, name):
+            tile = sb.tile([P, PACK, P], U8, name=name, align_bytes=64)
+            nc.gpsimd.memset(tile[:].bitcast(I32), 0)
+            for q in range(4):
+                rows = slice(first_row + 4 * q, first_row + 4 * q + 4)
+                nc.sync.dma_start(out=tile[32 * q : 32 * q + 4, :, :].bitcast(I32), in_=ws_dealt[rows, :, :].bitcast(I32))
+            return tile
+
+        w2 = (w2_dealt, placed_scales(68, "w2_plane"))
+        w3 = (w3_dealt, placed_scales(4, "w3_plane"))
+        w4 = (w4_dealt, placed_scales(36, "w4_plane"))
+
         res_t = sb.tile([P, PACK, S], F32, name="res_t", tag="big")
         nc.sync.dma_start(out=res_t[:], in_=res.rearrange("(p t) j -> p t j", t=PACK))
 
@@ -114,61 +142,82 @@ def tile_picked_midsoftbpolar_none_po_kernel(
             y_t = sb.tile([P, S], F32, name=f"y{t}")
             nc.scalar.copy(y_t[:], bank[:])
             y.append(y_t)
-        tanh_d = sb.tile([P, PACK, S], F32, name="tanh_d")
+
         d_banks = []
+        gd = []
         for t in range(PACK):
             bank = psum.tile([P, S], F32, name=f"d_bank{t}", tag=f"bank{PACK + t}")
             product(bank[:], w2, t, xb_words[:], xb_scales[:])
-            nc.scalar.activation(tanh_d[:, t, :], bank[:], ACT.Tanh)
+            gd_t = sb.tile([P, S], F32, name=f"gd{t}")
+            nc.scalar.activation(gd_t[:], bank[:], ACT.Copy, scale=gain[:, t : t + 1])
             d_banks.append(bank)
+            gd.append(gd_t)
 
         half_a = sb.tile([P, PACK, W], F32, name="half_a")
         pb = sb.tile([P, PACK, W], F32, name="pb")
         for t in range(PACK):
             nc.vector.tensor_scalar(half_a[:, t, :], y[t][:].indirect(n1_t[:]), -0.5, 0.0, ALU.mult, ALU.add)
             nc.vector.tensor_copy(pb[:, t, :], y[t][:].indirect(n2_t[:]))
-        w3 = deal_weight(w3_raw, "w3")
-        w4 = deal_weight(w4_raw, "w4")
 
-        sq_a = sb.tile([P, PACK, W], F32, name="sq_a")
-        sq_b = sb.tile([P, PACK, W], F32, name="sq_b")
-        nc.scalar.activation(sq_a[:], half_a[:], ACT.Square, scale=2.0)
-        nc.scalar.activation(sq_b[:], pb[:], ACT.Square)
+        sum_banks = []
+        squares = sb.tile([P, 2, 2, 2 * W], F32, name="squares", tag="xb_words", align_bytes=64)
+        for u in range(2):
+            planes = slice(2 * u, 2 * u + 2)
+            sq_a = squares[:, u, 0, :]
+            sq_b = squares[:, u, 1, :]
+            nc.scalar.activation(sq_a, half_a[:, planes, :].rearrange("p t c -> p (t c)"), ACT.Square, scale=2.0)
+            nc.scalar.activation(sq_b, pb[:, planes, :].rearrange("p t c -> p (t c)"), ACT.Square)
+            bank = psum.tile([P, S], F32, name=f"sum_bank{u}", tag=f"bank{u}")
+            for j in range(PACK):
+                block = slice(j * P, (j + 1) * P)
+                nc.tensor.matmul(bank[:, block], sq_a[:, block], identity[:], start=True, stop=False, is_transpose=True)
+                nc.tensor.matmul(bank[:, block], sq_b[:, block], identity[:], start=False, stop=True, is_transpose=True)
+            sum_banks.append(bank)
+        ra = sb.tile([P, PACK, W], F32, name="ra")
+        ra_banks = []
+        for u in range(2):
+            ra_turned = sb.tile([P, S], F32, name=f"ra_turned{u}", tag=f"turned{u}")
+            nc.scalar.activation(ra_turned[:], sum_banks[u][:], ACT.Sqrt, bias=quarter[:])
+            bank = psum.tile([P, S], F32, name=f"ra_bank{u}", tag=f"bank{2 + u}")
+            for j in range(PACK):
+                block = slice(j * P, (j + 1) * P)
+                nc.tensor.transpose(bank[:, block], ra_turned[:, block], identity[:])
+            ra_banks.append(bank)
+        for u in range(2):
+            nc.scalar.copy(ra[:, 2 * u : 2 * u + 2, :].rearrange("p t c -> p (t c)"), ra_banks[u][:])
 
-        dt = [sb.tile([P, S], F32, name=f"dt{t}") for t in range(PACK)]
-        sq = sb.tile([P, PACK, W], F32, name="sq")
-        ra = sb.tile([P, PACK, W], F32, name="ra", tag="ra_u")
+        tanh_d = sb.tile([P, PACK, S], F32, name="tanh_d", tag="turned1")
         for t in range(PACK):
-            nc.vector.tensor_tensor(dt[t][:].indirect(n2_t[:]), pb[:, t, :], half_a[:, t, :], ALU.add)
-            if t == 1:
-                nc.vector.scalar_tensor_tensor(sq[:], sq_a[:], 0.25, sq_b[:], ALU.add, ALU.add)
-                nc.scalar.activation(ra[:], sq[:], ACT.Sqrt)
-        gd = []
-        for t in range(PACK):
-            gd_t = sb.tile([P, S], F32, name=f"gd{t}")
-            nc.scalar.activation(gd_t[:], d_banks[t][:], ACT.Copy, scale=gain[:, t : t + 1])
-            gd.append(gd_t)
+            nc.scalar.activation(tanh_d[:, t, :], d_banks[t][:], ACT.Tanh)
 
-        z = sb.tile([P, S, PACK], BF16, name="z", tag="z_u", align_bytes=64)
+        dt = []
+        for t in range(PACK):
+            dt_t = sb.tile([P, S], F32, name=f"dt{t}", tag=("w2_plane", "xb_scales", "w2_dealt", "ws_dealt")[t], align_bytes=64)
+            nc.vector.tensor_tensor(dt_t[:].indirect(n2_t[:]), pb[:, t, :], half_a[:, t, :], ALU.add)
+            dt.append(dt_t)
+        z_pairs = sb.tile([P, 2, S, 2], BF16, name="z_pairs")
         for t in range(PACK):
             nc.vector.tensor_copy(dt[t][:].indirect(n1_t[:]), ra[:, t, :])
-            nc.scalar.activation(z[:, :, t], dt[t][:], ACT.Copy, scale=gain[:, t : t + 1])
+            nc.scalar.activation(z_pairs[:, t // 2, :, t % 2], dt[t][:], ACT.Copy, scale=gain[:, t : t + 1])
+        z = sb.tile([P, S * PACK], BF16, name="z", align_bytes=64)
+        nc.scalar.copy(
+            out=z[:].bitcast(F32).rearrange("p (c i u) -> p c u i", i=4, u=2),
+            in_=z_pairs[:].rearrange("p u c e -> p (u c e)").bitcast(F32).rearrange("p (u c i) -> p c u i", u=2, i=4),
+        )
 
-        def gated(dst, t):
-            for c in range(0, S, W):
+        def gated(c0, tag):
+            tile = sb.tile([P, PACK, W], F32, name=f"u{c0}", tag=tag)
+            for t in range(PACK):
                 nc.vector.tensor_tensor(
-                    dst[:, c : c + W], gd[t][:].indirect(n4_t[:, c // 16 : (c + W) // 16]), tanh_d[:, t, c : c + W], ALU.mult
+                    tile[:, t, :], gd[t][:].indirect(n4_t[:, c0 // 16 : (c0 + W) // 16]), tanh_d[:, t, c0 : c0 + W], ALU.mult
                 )
+            return tile
 
-        u_first = sb.tile([P, S], F32, name="u_first", tag="ra_u")
-        gated(u_first, 0)
+        u_first = gated(0, "u_first")
         z_codes = sb.tile([P, S], U32, name="z_codes", align_bytes=64)
         z_scales = sb.tile([P, S], U8, name="z_scales", align_bytes=64)
-        nc.vector.quantize_mx(out=z_codes[:].bitcast(FP8X4), scales=z_scales[:], in_=z[:].rearrange("p j t -> p (j t)"))
-        u_rest = sb.tile([P, PACK - 1, S], F32, name="u_rest", tag="z_u", align_bytes=64)
-        u = [u_first[:]] + [u_rest[:, t, :] for t in range(PACK - 1)]
-        for t in range(1, PACK):
-            gated(u[t], t)
+        nc.vector.quantize_mx(out=z_codes[:].bitcast(FP8X4), scales=z_scales[:], in_=z[:])
+        u_halves = (u_first, gated(W, "z_pairs"))
 
         gh = []
         for t in range(PACK):
@@ -186,10 +235,10 @@ def tile_picked_midsoftbpolar_none_po_kernel(
             last = index == len(CHUNKS) - 1
             copy = nc.vector.tensor_copy if last else nc.scalar.copy
             cols = slice(c0, c0 + n)
-            z2f = sb.tile([P, PACK, n], F32, name=f"z2f{index}")
+            z2f = sb.tile([P, PACK, n], F32, name=f"z2f{index}", tag=("z2f", "gain", "z2f")[index])
             for t in range(PACK):
                 nc.vector.tensor_tensor(
-                    z2f[:, t, :], gh[t][:].indirect(n3_t[:, c0 // 16 : (c0 + n) // 16]), u[t][:, cols], ALU.subtract
+                    z2f[:, t, :], gh[t][:].indirect(n3_t[:, c0 // 16 : (c0 + n) // 16]), u_halves[c0 // W][:, t, c0 % W : c0 % W + n], ALU.subtract
                 )
             z2 = sb.tile([P, n, PACK], BF16, name=f"z2{index}", align_bytes=64)
             interleave(copy, z2[:], z2f[:])

@@ -74,7 +74,7 @@ def tile_picked_midsoftbpolar_none_po_kernel(
             )
 
         def interleave(copy, dst, src):
-            copy(out=dst.rearrange("p (c i) t -> p c t i", i=4), in_=src.rearrange("p t (c i) -> p c t i", i=4))
+            copy(out=dst.rearrange("p (c i) t -> p c t i", i=2), in_=src.rearrange("p t (c i) -> p c t i", i=2))
 
         offs_t = load_list(offs, "offs_t")
         w1_raw = load_words(w1_words, "w1_raw")
@@ -102,8 +102,6 @@ def tile_picked_midsoftbpolar_none_po_kernel(
 
         quarter = sb.tile([P, 1], F32, name="quarter")
         nc.gpsimd.memset(quarter[:], 0.25)
-        warm = sb.tile([P, 1], F32, name="warm")
-        nc.scalar.activation(warm[:], quarter[:], ACT.Sqrt)
 
         xa_scales = sb.tile([P, S], U8, name="xa_scales", align_bytes=64)
         xa_words = sb.tile([P, S], U32, name="xa_words", align_bytes=64)
@@ -144,14 +142,12 @@ def tile_picked_midsoftbpolar_none_po_kernel(
             y.append(y_t)
 
         d_banks = []
-        gd = []
+        tanh_d = sb.tile([P, PACK, S], F32, name="tanh_d")
         for t in range(PACK):
             bank = psum.tile([P, S], F32, name=f"d_bank{t}", tag=f"bank{PACK + t}")
             product(bank[:], w2, t, xb_words[:], xb_scales[:])
-            gd_t = sb.tile([P, S], F32, name=f"gd{t}")
-            nc.scalar.activation(gd_t[:], bank[:], ACT.Copy, scale=gain[:, t : t + 1])
+            nc.scalar.activation(tanh_d[:, t, :], bank[:], ACT.Tanh)
             d_banks.append(bank)
-            gd.append(gd_t)
 
         half_a = sb.tile([P, PACK, W], F32, name="half_a")
         pb = sb.tile([P, PACK, W], F32, name="pb")
@@ -176,7 +172,7 @@ def tile_picked_midsoftbpolar_none_po_kernel(
         ra = sb.tile([P, PACK, W], F32, name="ra")
         ra_banks = []
         for u in range(2):
-            ra_turned = sb.tile([P, S], F32, name=f"ra_turned{u}", tag=f"turned{u}")
+            ra_turned = sb.tile([P, S], F32, name=f"ra_turned{u}")
             nc.scalar.activation(ra_turned[:], sum_banks[u][:], ACT.Sqrt, bias=quarter[:])
             bank = psum.tile([P, S], F32, name=f"ra_bank{u}", tag=f"bank{2 + u}")
             for j in range(PACK):
@@ -186,16 +182,18 @@ def tile_picked_midsoftbpolar_none_po_kernel(
         for u in range(2):
             nc.scalar.copy(ra[:, 2 * u : 2 * u + 2, :].rearrange("p t c -> p (t c)"), ra_banks[u][:])
 
-        tanh_d = sb.tile([P, PACK, S], F32, name="tanh_d", tag="turned1")
+        gd = []
         for t in range(PACK):
-            nc.scalar.activation(tanh_d[:, t, :], d_banks[t][:], ACT.Tanh)
+            gd_t = sb.tile([P, S], F32, name=f"gd{t}")
+            nc.scalar.activation(gd_t[:], d_banks[t][:], ACT.Copy, scale=gain[:, t : t + 1])
+            gd.append(gd_t)
 
         dt = []
         for t in range(PACK):
             dt_t = sb.tile([P, S], F32, name=f"dt{t}", tag=("w2_plane", "xb_scales", "w2_dealt", "ws_dealt")[t], align_bytes=64)
             nc.vector.tensor_tensor(dt_t[:].indirect(n2_t[:]), pb[:, t, :], half_a[:, t, :], ALU.add)
             dt.append(dt_t)
-        z_pairs = sb.tile([P, 2, S, 2], BF16, name="z_pairs")
+        z_pairs = sb.tile([P, 2, S, 2], BF16, name="z_pairs", align_bytes=64)
         for t in range(PACK):
             nc.vector.tensor_copy(dt[t][:].indirect(n1_t[:]), ra[:, t, :])
             nc.scalar.activation(z_pairs[:, t // 2, :, t % 2], dt[t][:], ACT.Copy, scale=gain[:, t : t + 1])
@@ -206,14 +204,14 @@ def tile_picked_midsoftbpolar_none_po_kernel(
         )
 
         def gated(c0, tag):
-            tile = sb.tile([P, PACK, W], F32, name=f"u{c0}", tag=tag)
+            tile = sb.tile([P, PACK, W], F32, name=f"u{c0}", tag=tag, align_bytes=64)
             for t in range(PACK):
                 nc.vector.tensor_tensor(
                     tile[:, t, :], gd[t][:].indirect(n4_t[:, c0 // 16 : (c0 + W) // 16]), tanh_d[:, t, c0 : c0 + W], ALU.mult
                 )
             return tile
 
-        u_first = gated(0, "u_first")
+        u_first = gated(0, "w2_plane")
         z_codes = sb.tile([P, S], U32, name="z_codes", align_bytes=64)
         z_scales = sb.tile([P, S], U8, name="z_scales", align_bytes=64)
         nc.vector.quantize_mx(out=z_codes[:].bitcast(FP8X4), scales=z_scales[:], in_=z[:])

@@ -228,39 +228,66 @@ def tile_picked_midsoftbpolar_none_po_kernel(
         out_scales = sb.tile([P, S], U8, name="out_scales", align_bytes=64)
         out_rows = out_0.rearrange("(p t) j -> p t j", t=PACK)
         out_words = out_1[0].rearrange("p n t -> p (n t)").bitcast(I32)
-        next_bank = PACK
-        for index, (c0, n) in enumerate(CHUNKS):
-            last = index == len(CHUNKS) - 1
-            copy = nc.vector.tensor_copy if last else nc.scalar.copy
-            cols = slice(c0, c0 + n)
-            z2f = sb.tile([P, PACK, n], F32, name=f"z2f{index}", tag=("z2f", "gain", "z2f")[index])
+        def fetch(index, tag):
+            c0, n = CHUNKS[index]
+            z2_rows = sb.tile([P, PACK, n], F32, name=f"z2_rows{index}", tag=tag)
             for t in range(PACK):
                 nc.vector.tensor_tensor(
-                    z2f[:, t, :], gh[t][:].indirect(n3_t[:, c0 // 16 : (c0 + n) // 16]), u_halves[c0 // W][:, t, c0 % W : c0 % W + n], ALU.subtract
+                    z2_rows[:, t, :], gh[t][:].indirect(n3_t[:, c0 // 16 : (c0 + n) // 16]),
+                    u_halves[c0 // W][:, t, c0 % W : c0 % W + n], ALU.subtract,
                 )
             z2 = sb.tile([P, n, PACK], BF16, name=f"z2{index}", align_bytes=64)
-            interleave(copy, z2[:], z2f[:])
+            interleave(nc.scalar.copy, z2[:], z2_rows[:])
+            return z2
+
+        def multiply(index, z2, first_bank):
+            n = CHUNKS[index][1]
             z2_codes = sb.tile([P, n], U32, name=f"z2_codes{index}", align_bytes=64)
             z2_scales = sb.tile([P, n], U8, name=f"z2_scales{index}", align_bytes=64)
             nc.vector.quantize_mx(out=z2_codes[:].bitcast(FP8X4), scales=z2_scales[:], in_=z2[:].rearrange("p j t -> p (j t)"))
-            result = sb.tile([P, PACK, n], F32, name=f"result{index}")
             per_bank = S // n
+            banks = []
             for t0 in range(0, PACK, per_bank):
-                bank = psum.tile([P, per_bank, n], F32, name=f"o_bank{index}_{t0}", tag=f"bank{next_bank}")
-                next_bank = next_bank + 1
+                bank = psum.tile([P, per_bank, n], F32, name=f"o_bank{index}_{t0}", tag=f"bank{first_bank + len(banks)}")
                 for t in range(t0, t0 + per_bank):
                     product(bank[:, t - t0, :], w4, t, z2_codes[:], z2_scales[:])
-                nc.vector.tensor_tensor(
-                    result[:, t0 : t0 + per_bank, :], bank[:], res_t[:, t0 : t0 + per_bank, cols], ALU.add
-                )
+                banks.append(bank)
+            return banks
+
+        def add_residual(index, banks, copy):
+            c0, n = CHUNKS[index]
+            cols = slice(c0, c0 + n)
+            result = sb.tile([P, PACK, n], F32, name=f"result{index}")
+            per_bank = S // n
+            for b, bank in enumerate(banks):
+                planes = slice(b * per_bank, (b + 1) * per_bank)
+                nc.vector.tensor_tensor(result[:, planes, :], bank[:], res_t[:, planes, cols], ALU.add)
             nc.sync.dma_start(out=out_rows[:, :, cols], in_=result[:])
             rounded = sb.tile([P, n, PACK], BF16, name=f"rounded{index}", align_bytes=64)
             interleave(copy, rounded[:], result[:])
+            return rounded
+
+        def hand_on(index, rounded):
+            c0, n = CHUNKS[index]
+            cols = slice(c0, c0 + n)
             out_codes = sb.tile([P, n], U32, name=f"out_codes{index}", align_bytes=64)
             nc.vector.quantize_mx(
                 out=out_codes[:].bitcast(FP8X4), scales=out_scales[:, cols], in_=rounded[:].rearrange("p j t -> p (j t)")
             )
             nc.sync.dma_start(out=out_words[:, cols], in_=out_codes[:].bitcast(I32))
+
+        z2_first = fetch(0, "z2_rows")
+        z2_second = fetch(1, "gain")
+        banks_first = multiply(0, z2_first, PACK)
+        z2_third = fetch(2, "z2_rows")
+        banks_second = multiply(1, z2_second, PACK + 2)
+        banks_third = multiply(2, z2_third, PACK + 3)
+        rounded_first = add_residual(0, banks_first, nc.scalar.copy)
+        rounded_second = add_residual(1, banks_second, nc.scalar.copy)
+        rounded_third = add_residual(2, banks_third, nc.vector.tensor_copy)
+        hand_on(0, rounded_first)
+        hand_on(1, rounded_second)
+        hand_on(2, rounded_third)
         for q in range(4):
             queue = nc.sync if q % 2 == 0 else nc.scalar
             queue.dma_start(

from contextlib import ExitStack

import concourse.mybir as mybir
from concourse.masks import make_identity

F32 = mybir.dt.float32
BF16 = mybir.dt.bfloat16
I32 = mybir.dt.int32
U32 = mybir.dt.uint32
U16 = mybir.dt.uint16
U8 = mybir.dt.uint8
FP8X4 = mybir.dt.float8_e4m3fn_x4
FP4X4 = mybir.dt.float4_e2m1fn_x4
ACT = mybir.ActivationFunctionType
ALU = mybir.AluOpType

P = 128
PACK = 4
T = 2048
S = 512
W = 256
FLOPS = 4 * 2 * 512 * 512 * 512
CHUNKS = ((0, 256), (256, 128), (384, 128))


def tile_picked_midsoftbpolar_none_po_kernel(
    tc, x_words, x_scales, w1_words, w1_scales, w2_words, w2_scales, gn, w3_words, w3_scales, res,
    w4_words, w4_scales, offs, two, n1, n2, n3, n4, out_0, out_1, out_2,
):
    nc = tc.nc
    with ExitStack() as ctx:
        lists = ctx.enter_context(tc.tile_pool(name="lists", bufs=1))
        sb = ctx.enter_context(tc.tile_pool(name="sb", bufs=1))
        psum = ctx.enter_context(tc.psum_pool(name="psum", bufs=1))

        def load_list(src, name):
            tile = lists.tile(list(src.shape), U16, name=name)
            nc.sync.dma_start(tile[:], src)
            return tile

        def load_scale_rows(tile, src):
            for q in range(4):
                nc.sync.dma_start(
                    out=tile[32 * q : 32 * q + 4, :].bitcast(I32), in_=src[0, 4 * q : 4 * q + 4, :].bitcast(I32)
                )

        def load_words(src, name):
            tile = sb.tile([P, 2 * S], U8, name=name, align_bytes=64)
            nc.sync.dma_start(out=tile[:].bitcast(I32), in_=src[0].bitcast(I32))
            return tile

        def zeroed(name, width):
            tile = sb.tile([P, width], U8, name=name, align_bytes=64)
            nc.gpsimd.memset(tile[:].bitcast(I32), 0)
            return tile

        def deal_words(raw, name):
            words = sb.tile([P, PACK, 2 * P], U8, name=name, align_bytes=64)
            nc.vector.tensor_copy(
                out=words[:].rearrange("p t (m b) -> p t m b", b=2),
                in_=raw[:].rearrange("p (m t b) -> p t m b", t=PACK, b=2),
            )
            return words

        def deal_scales(raw, name):
            scales = sb.tile([P, PACK, P], U8, name=name, align_bytes=64)
            nc.vector.tensor_copy(out=scales[:], in_=raw[:].rearrange("p (m t) -> p t m", t=PACK))
            return scales

        def product(out, weight, t, codes, scales):
            nc.tensor.matmul_mx(
                out=out, lhsT=weight[0][:, t, :].bitcast(FP4X4), lhsT_scale=weight[1][:, t, :],
                rhs=codes.bitcast(FP8X4), rhs_scale=scales, start=True, stop=True,
            )

        def interleave(copy, dst, src):
            copy(out=dst.rearrange("p (c i) t -> p c t i", i=2), in_=src.rearrange("p t (c i) -> p c t i", i=2))

        offs_t = load_list(offs, "offs_t")
        w1_raw = load_words(w1_words, "w1_raw")
        w2_raw = load_words(w2_words, "w2_raw")
        w3_raw = load_words(w3_words, "w3_raw")
        w4_raw = load_words(w4_words, "w4_raw")
        xw = sb.tile([P, T], U32, name="xw", tag="big")
        nc.sync.dma_start(out=xw[:].bitcast(I32), in_=x_words[0].rearrange("p n t -> p (n t)").bitcast(I32))
        xs = zeroed("xs", T)
        load_scale_rows(xs, x_scales)
        ws_raw = zeroed("ws_raw", S)
        load_scale_rows(ws_raw, w1_scales)
        nc.sync.dma_start(out=ws_raw[68:84, :].bitcast(I32), in_=w2_scales[0].bitcast(I32))
        nc.sync.dma_start(out=ws_raw[4:20, :].bitcast(I32), in_=w3_scales[0].bitcast(I32))
        nc.sync.dma_start(out=ws_raw[36:52, :].bitcast(I32), in_=w4_scales[0].bitcast(I32))
        two_t = load_list(two, "two_t")
        n1_t = load_list(n1, "n1_t")
        n2_t = load_list(n2, "n2_t")
        gain = sb.tile([P, PACK], F32, name="gain")
        nc.sync.dma_start(out=gain[:], in_=gn.rearrange("(p t) o -> p (t o)", t=PACK))
        n3_t = load_list(n3, "n3_t")
        n4_t = load_list(n4, "n4_t")
        identity = sb.tile([P, P], F32, name="identity")
        make_identity(nc, identity[:])

        quarter = sb.tile([P, 1], F32, name="quarter")
        nc.gpsimd.memset(quarter[:], 0.25)

        xa_scales = sb.tile([P, S], U8, name="xa_scales", align_bytes=64)
        xa_words = sb.tile([P, S], U32, name="xa_words", align_bytes=64)
        w1_dealt = deal_words(w1_raw, "w1_dealt")
        w2_dealt = deal_words(w2_raw, "w2_dealt")
        w3_dealt = deal_words(w3_raw, "w3_dealt")
        w4_dealt = deal_words(w4_raw, "w4_dealt")
        nc.vector.tensor_copy(xa_words[:], xw[:].indirect(offs_t[:]))
        nc.vector.tensor_copy(xa_scales[:], xs[:].indirect(offs_t[:]))
        ws_dealt = deal_scales(ws_raw, "ws_dealt")
        w1 = (w1_dealt, ws_dealt)
        xb_scales = sb.tile([P, S], U8, name="xb_scales", align_bytes=64)
        nc.vector.tensor_copy(xb_scales[:], xs[:].indirect(two_t[:]))
        xb_words = sb.tile([P, S], U32, name="xb_words", align_bytes=64)
        nc.vector.tensor_copy(xb_words[:], xw[:].indirect(two_t[:]))

        def placed_scales(first_row, name):
            tile = sb.tile([P, PACK, P], U8, name=name, align_bytes=64)
            nc.gpsimd.memset(tile[:].bitcast(I32), 0)
            for q in range(4):
                rows = slice(first_row + 4 * q, first_row + 4 * q + 4)
                nc.sync.dma_start(out=tile[32 * q : 32 * q + 4, :, :].bitcast(I32), in_=ws_dealt[rows, :, :].bitcast(I32))
            return tile

        w2 = (w2_dealt, placed_scales(68, "w2_plane"))
        w3 = (w3_dealt, placed_scales(4, "w3_plane"))
        w4 = (w4_dealt, placed_scales(36, "w4_plane"))

        res_t = sb.tile([P, PACK, S], F32, name="res_t", tag="big")
        nc.sync.dma_start(out=res_t[:], in_=res.rearrange("(p t) j -> p t j", t=PACK))

        y = []
        for t in range(PACK):
            bank = psum.tile([P, S], F32, name=f"y_bank{t}", tag=f"bank{t}")
            product(bank[:], w1, t, xa_words[:], xa_scales[:])
            y_t = sb.tile([P, S], F32, name=f"y{t}")
            nc.scalar.copy(y_t[:], bank[:])
            y.append(y_t)

        d_banks = []
        tanh_d = sb.tile([P, PACK, S], F32, name="tanh_d")
        for t in range(PACK):
            bank = psum.tile([P, S], F32, name=f"d_bank{t}", tag=f"bank{PACK + t}")
            product(bank[:], w2, t, xb_words[:], xb_scales[:])
            nc.scalar.activation(tanh_d[:, t, :], bank[:], ACT.Tanh)
            d_banks.append(bank)

        half_a = sb.tile([P, PACK, W], F32, name="half_a")
        pb = sb.tile([P, PACK, W], F32, name="pb")
        for t in range(PACK):
            nc.vector.tensor_scalar(half_a[:, t, :], y[t][:].indirect(n1_t[:]), -0.5, 0.0, ALU.mult, ALU.add)
            nc.vector.tensor_copy(pb[:, t, :], y[t][:].indirect(n2_t[:]))

        sum_banks = []
        squares = sb.tile([P, 2, 2, 2 * W], F32, name="squares", tag="xb_words", align_bytes=64)
        for u in range(2):
            planes = slice(2 * u, 2 * u + 2)
            sq_a = squares[:, u, 0, :]
            sq_b = squares[:, u, 1, :]
            nc.scalar.activation(sq_a, half_a[:, planes, :].rearrange("p t c -> p (t c)"), ACT.Square, scale=2.0)
            nc.scalar.activation(sq_b, pb[:, planes, :].rearrange("p t c -> p (t c)"), ACT.Square)
            bank = psum.tile([P, S], F32, name=f"sum_bank{u}", tag=f"bank{u}")
            for j in range(PACK):
                block = slice(j * P, (j + 1) * P)
                nc.tensor.matmul(bank[:, block], sq_a[:, block], identity[:], start=True, stop=False, is_transpose=True)
                nc.tensor.matmul(bank[:, block], sq_b[:, block], identity[:], start=False, stop=True, is_transpose=True)
            sum_banks.append(bank)
        ra = sb.tile([P, PACK, W], F32, name="ra")
        ra_banks = []
        for u in range(2):
            ra_turned = sb.tile([P, S], F32, name=f"ra_turned{u}")
            nc.scalar.activation(ra_turned[:], sum_banks[u][:], ACT.Sqrt, bias=quarter[:])
            bank = psum.tile([P, S], F32, name=f"ra_bank{u}", tag=f"bank{2 + u}")
            for j in range(PACK):
                block = slice(j * P, (j + 1) * P)
                nc.tensor.transpose(bank[:, block], ra_turned[:, block], identity[:])
            ra_banks.append(bank)
        for u in range(2):
            nc.scalar.copy(ra[:, 2 * u : 2 * u + 2, :].rearrange("p t c -> p (t c)"), ra_banks[u][:])

        gd = []
        for t in range(PACK):
            gd_t = sb.tile([P, S], F32, name=f"gd{t}")
            nc.scalar.activation(gd_t[:], d_banks[t][:], ACT.Copy, scale=gain[:, t : t + 1])
            gd.append(gd_t)

        dt = []
        for t in range(PACK):
            dt_t = sb.tile([P, S], F32, name=f"dt{t}", tag=("w2_plane", "xb_scales", "w2_dealt", "ws_dealt")[t], align_bytes=64)
            nc.vector.tensor_tensor(dt_t[:].indirect(n2_t[:]), pb[:, t, :], half_a[:, t, :], ALU.add)
            dt.append(dt_t)
        z_pairs = sb.tile([P, 2, S, 2], BF16, name="z_pairs", align_bytes=64)
        for t in range(PACK):
            nc.vector.tensor_copy(dt[t][:].indirect(n1_t[:]), ra[:, t, :])
            nc.scalar.activation(z_pairs[:, t // 2, :, t % 2], dt[t][:], ACT.Copy, scale=gain[:, t : t + 1])
        z = sb.tile([P, S * PACK], BF16, name="z", align_bytes=64)
        nc.scalar.copy(
            out=z[:].bitcast(F32).rearrange("p (c i u) -> p c u i", i=4, u=2),
            in_=z_pairs[:].rearrange("p u c e -> p (u c e)").bitcast(F32).rearrange("p (u c i) -> p c u i", u=2, i=4),
        )

        def gated(c0, tag):
            tile = sb.tile([P, PACK, W], F32, name=f"u{c0}", tag=tag, align_bytes=64)
            for t in range(PACK):
                nc.vector.tensor_tensor(
                    tile[:, t, :], gd[t][:].indirect(n4_t[:, c0 // 16 : (c0 + W) // 16]), tanh_d[:, t, c0 : c0 + W], ALU.mult
                )
            return tile

        u_first = gated(0, "w2_plane")
        z_codes = sb.tile([P, S], U32, name="z_codes", align_bytes=64)
        z_scales = sb.tile([P, S], U8, name="z_scales", align_bytes=64)
        nc.vector.quantize_mx(out=z_codes[:].bitcast(FP8X4), scales=z_scales[:], in_=z[:])
        u_halves = (u_first, gated(W, "z_pairs"))

        gh = []
        for t in range(PACK):
            bank = psum.tile([P, S], F32, name=f"h_bank{t}", tag=f"bank{t}")
            product(bank[:], w3, t, z_codes[:], z_scales[:])
            gh_t = sb.tile([P, S], F32, name=f"gh{t}")
            nc.scalar.activation(gh_t[:], bank[:], ACT.Copy, scale=gain[:, t : t + 1])
            gh.append(gh_t)

        out_scales = sb.tile([P, S], U8, name="out_scales", align_bytes=64)
        out_rows = out_0.rearrange("(p t) j -> p t j", t=PACK)
        out_words = out_1[0].rearrange("p n t -> p (n t)").bitcast(I32)
        def fetch(index, tag):
            c0, n = CHUNKS[index]
            z2_rows = sb.tile([P, PACK, n], F32, name=f"z2_rows{index}", tag=tag)
            for t in range(PACK):
                nc.vector.tensor_tensor(
                    z2_rows[:, t, :], gh[t][:].indirect(n3_t[:, c0 // 16 : (c0 + n) // 16]),
                    u_halves[c0 // W][:, t, c0 % W : c0 % W + n], ALU.subtract,
                )
            z2 = sb.tile([P, n, PACK], BF16, name=f"z2{index}", align_bytes=64)
            interleave(nc.scalar.copy, z2[:], z2_rows[:])
            return z2

        def multiply(index, z2, first_bank):
            n = CHUNKS[index][1]
            z2_codes = sb.tile([P, n], U32, name=f"z2_codes{index}", align_bytes=64)
            z2_scales = sb.tile([P, n], U8, name=f"z2_scales{index}", align_bytes=64)
            nc.vector.quantize_mx(out=z2_codes[:].bitcast(FP8X4), scales=z2_scales[:], in_=z2[:].rearrange("p j t -> p (j t)"))
            per_bank = S // n
            banks = []
            for t0 in range(0, PACK, per_bank):
                bank = psum.tile([P, per_bank, n], F32, name=f"o_bank{index}_{t0}", tag=f"bank{first_bank + len(banks)}")
                for t in range(t0, t0 + per_bank):
                    product(bank[:, t - t0, :], w4, t, z2_codes[:], z2_scales[:])
                banks.append(bank)
            return banks

        def add_residual(index, banks, copy):
            c0, n = CHUNKS[index]
            cols = slice(c0, c0 + n)
            result = sb.tile([P, PACK, n], F32, name=f"result{index}")
            per_bank = S // n
            for b, bank in enumerate(banks):
                planes = slice(b * per_bank, (b + 1) * per_bank)
                nc.vector.tensor_tensor(result[:, planes, :], bank[:], res_t[:, planes, cols], ALU.add)
            nc.sync.dma_start(out=out_rows[:, :, cols], in_=result[:])
            rounded = sb.tile([P, n, PACK], BF16, name=f"rounded{index}", align_bytes=64)
            interleave(copy, rounded[:], result[:])
            return rounded

        def hand_on(index, rounded):
            c0, n = CHUNKS[index]
            cols = slice(c0, c0 + n)
            out_codes = sb.tile([P, n], U32, name=f"out_codes{index}", align_bytes=64)
            nc.vector.quantize_mx(
                out=out_codes[:].bitcast(FP8X4), scales=out_scales[:, cols], in_=rounded[:].rearrange("p j t -> p (j t)")
            )
            nc.sync.dma_start(out=out_words[:, cols], in_=out_codes[:].bitcast(I32))

        z2_first = fetch(0, "z2_rows")
        z2_second = fetch(1, "gain")
        banks_first = multiply(0, z2_first, PACK)
        z2_third = fetch(2, "z2_rows")
        banks_second = multiply(1, z2_second, PACK + 2)
        banks_third = multiply(2, z2_third, PACK + 3)
        rounded_first = add_residual(0, banks_first, nc.scalar.copy)
        rounded_second = add_residual(1, banks_second, nc.scalar.copy)
        rounded_third = add_residual(2, banks_third, nc.vector.tensor_copy)
        hand_on(0, rounded_first)
        hand_on(1, rounded_second)
        hand_on(2, rounded_third)
        for q in range(4):
            queue = nc.sync if q % 2 == 0 else nc.scalar
            queue.dma_start(
                out=out_2[0, 4 * q : 4 * q + 4, :].bitcast(I32), in_=out_scales[32 * q : 32 * q + 4, :].bitcast(I32)
            )
